import numpy as np
import ml_dtypes


def mxq(x, axis, fmt="e4m3"):
    dtype, down = {"e4m3": (ml_dtypes.float8_e4m3fn, 7), "e5m2": (ml_dtypes.float8_e5m2, 14)}[fmt]
    v = np.moveaxis(np.asarray(x, np.float32).astype(ml_dtypes.bfloat16).astype(np.float64), axis, -1)
    blocks = v.reshape(v.shape[:-1] + (-1, 32))
    amax = np.abs(blocks).max(-1, keepdims=True)
    byte = np.maximum(np.where(amax > 0, np.frexp(amax)[1] - 1 + 127, 0) - down, 1)
    scale = np.exp2(byte - 127.0)
    codes = (blocks / scale).astype(np.float32).astype(dtype).astype(np.float64)
    return np.moveaxis((codes * scale).reshape(v.shape), -1, axis)


WIDE = False


def mx_kscale(k):
    if not WIDE:
        return np.ones(k)
    levels = np.array([10, -10, 5, -5, 0])
    if k % 512:
        return np.exp2(np.random.permutation(np.resize(levels, k // 32))).repeat(32)
    a = np.empty((k // 512, 16))
    for p in range(k // 512):
        a[p, :8] = np.random.permutation(np.resize(levels, 8))
        for g in range(8):
            far = levels[np.abs(levels - a[p, g]) >= 10]
            a[p, g + 8] = far[np.random.randint(len(far))]
    return np.exp2(a.ravel()).repeat(32)


def f64(x):
    return np.asarray(x).astype(np.float64)


def striped(idx):
    return np.tile(idx.reshape(-1, 16).T, (8, 1)).astype(np.uint16)


def unstriped(offs):
    return offs[:16].T.reshape(-1).astype(np.int64)


def pack_weight(w):
    k, n = w.shape
    w = f64(np.asarray(w, np.float32).astype(ml_dtypes.bfloat16)).reshape(k // 32, 32, n)
    amax = np.abs(w).max(1)
    byte = np.clip(np.where(amax > 0, np.frexp(amax)[1] - 1 + 127 - 7, 1), 1, 254)
    scaled = (w * np.exp2(127.0 - byte)[:, None, :]).reshape(k, n).astype(np.float32)
    words = np.ascontiguousarray(scaled.reshape(k // 512, 128, 4, n).transpose(0, 1, 3, 2)).astype(ml_dtypes.float8_e4m3fn).view(np.uint8)
    return words, np.ascontiguousarray(byte.astype(np.uint8).reshape(k // 512, 16, n))


def unpack_weight(words, scales):
    g, p, n, _ = words.shape
    vals = np.ascontiguousarray(words).view(ml_dtypes.float8_e4m3fn).astype(np.float64) * np.repeat(np.exp2(scales.astype(np.float64) - 127.0), 8, axis=1)[..., None]
    return vals.transpose(0, 1, 3, 2).reshape(g * 512, n)


K, T, E, C, N = 512, 1024, 8, 256, 128


def by_expert(wq, xq):
    return np.concatenate([wq[e].T @ xq[:, e * C:(e + 1) * C] for e in range(E)], axis=1)


def setup_inputs():
    n = np.random.standard_normal
    s = mx_kscale(K)[:, None]
    first = np.random.permutation(np.repeat(np.arange(E), T // E))
    second = (first + 1 + np.random.permutation(np.repeat(np.arange(E - 1), -(-T // (E - 1)))[:T])) % E
    while np.bincount(second, minlength=E).max() != T // E:
        load = np.bincount(second, minlength=E); hi, lo = int(load.argmax()), int(load.argmin())
        t = np.flatnonzero((second == hi) & (first != lo))[0]; second[t] = lo
    slot_token = np.empty(E * C, np.int64); pos = np.empty((2, T), np.int64); fill = np.zeros(E, np.int64)
    place = np.stack([np.random.permutation(C) for _ in range(E)])
    for r, deal in enumerate((first, second)):
        for t in np.random.permutation(T):
            e = deal[t]; j = e * C + place[e, fill[e]]; fill[e] += 1; slot_token[j] = t; pos[r, t] = j
    g = np.random.uniform(0.2, 0.8, T)
    packed = [pack_weight(m) for m in n((E, K, N)) / np.sqrt(K) / s[None]]
    return {
        "xT": (n((K, T)) * s).astype(np.float32),
        "w_words": np.stack([m[0] for m in packed]),
        "w_scales": np.stack([m[1] for m in packed]),
        "gate": np.stack([np.tile(g, (N, 1)), np.tile(1.0 - g, (N, 1))]).astype(np.float32),
        "offs": striped(slot_token),
        "pos1": striped(pos[0]),
        "pos2": striped(pos[1]),
    }


def reference(xT, w_words, w_scales, gate, offs, pos1, pos2):
    idx = unstriped(offs)
    xq = mxq(f64(xT)[:, idx], 0, "e4m3")
    w = np.stack([unpack_weight(w_words[e], w_scales[e]) for e in range(E)])
    y = by_expert(w, xq)
    return f64(gate[0]) * y[:, unstriped(pos1)] + f64(gate[1]) * y[:, unstriped(pos2)]

@@ -1,0 +1,123 @@
+import concourse.mybir as mybir
+
+F32 = mybir.dt.float32
+BF16 = mybir.dt.bfloat16
+I32 = mybir.dt.int32
+U32 = mybir.dt.uint32
+U16 = mybir.dt.uint16
+U8 = mybir.dt.uint8
+FP8X4 = mybir.dt.float8_e4m3fn_x4
+MULT = mybir.AluOpType.mult
+ADD = mybir.AluOpType.add
+
+P = 128
+K, T, E, C, N = 512, 1024, 8, 256, 128
+SLOTS = E * C
+FLOPS = 2 * K * N * SLOTS
+
+LOADS = (256, 256, 256, 128, 128)
+SCALAR_SHARE = (96, 96, 96, 48, 48)
+SECOND = (512, 384, 128)
+
+
+def tile_routed_moe_kernel(tc, xT, w_words, w_scales, gate, offs, pos1, pos2, out):
+    nc = tc.nc
+    with (
+        tc.tile_pool(name="keep", bufs=1) as keep,
+        tc.psum_pool(name="psum", bufs=1) as psum,
+    ):
+        offs_sb = keep.tile([P, SLOTS // 16], U16, name="offs_sb")
+        pos1_sb = keep.tile([P, T // 16], U16, name="pos1_sb")
+        pos2_sb = keep.tile([P, T // 16], U16, name="pos2_sb")
+        x_words = keep.tile([P, T], U32, name="x_words", align_bytes=64)
+        x_scales = keep.tile([P, T], U8, name="x_scales", align_bytes=64)
+        w_codes = keep.tile([P, E, N], I32, name="w_codes", align_bytes=64)
+        w_bytes = keep.tile([P, E, N], U8, name="w_bytes", align_bytes=64)
+        gates = keep.tile([P, 2, T], F32, name="gates")
+        y = keep.tile([P, SLOTS], F32, name="y")
+        warm = keep.tile([P, 16], F32, name="warm")
+        warm2 = keep.tile([P, 16], F32, name="warm2")
+
+        nc.gpsimd.memset(warm[:], 0.0)
+        nc.scalar.copy(warm2[:], warm[:])
+        nc.gpsimd.memset(x_scales[:], 0)
+        nc.vector.memset(w_bytes[:].bitcast(I32), 0)
+
+        x_rows = xT.rearrange("(p t) n -> p t n", t=4)
+        t0 = 0
+        raws = []
+        for i, n in enumerate(LOADS):
+            raw = keep.tile([P, 4, n], F32, name="raw%d" % i)
+            nc.sync.dma_start(out=raw[:], in_=x_rows[:, :, t0:t0 + n])
+            raws.append(raw)
+            t0 += n
+        nc.sync.dma_start(offs_sb[:], offs)
+        nc.sync.dma_start(out=w_codes[:], in_=w_words[:, 0].rearrange("e p n r -> p e (n r)").bitcast(I32))
+        for q in range(4):
+            nc.sync.dma_start(
+                out=w_bytes[32 * q:32 * q + 4, :, :].bitcast(I32),
+                in_=w_scales[:, 0, 4 * q:4 * q + 4, :].rearrange("e q n -> q e n").bitcast(I32),
+            )
+        nc.sync.dma_start(pos1_sb[:], pos1)
+        nc.sync.dma_start(out=gates[:, 0, :], in_=gate[0])
+        nc.sync.dma_start(pos2_sb[:], pos2)
+        nc.sync.dma_start(out=gates[:, 1, :], in_=gate[1])
+
+        t0 = 0
+        for i, n in enumerate(LOADS):
+            pairs = keep.tile([P, n, 4], BF16, name="pairs%d" % i, align_bytes=64)
+            s = SCALAR_SHARE[i]
+            for copy, a, b in ((nc.scalar.copy, 0, s), (nc.vector.tensor_copy, s, n)):
+                if b > a:
+                    copy(
+                        out=pairs[:, a:b, :].rearrange("p (c i) t -> p c t i", i=4),
+                        in_=raws[i][:, :, a:b].rearrange("p t (c i) -> p c t i", i=4),
+                    )
+            nc.vector.quantize_mx(
+                out=x_words[:, t0:t0 + n].bitcast(FP8X4),
+                scales=x_scales[:, t0:t0 + n],
+                in_=pairs[:].rearrange("p n t -> p (n t)"),
+            )
+            t0 += n
+
+        words = keep.tile([P, SLOTS], U32, name="words", align_bytes=64)
+        scales = keep.tile([P, SLOTS], U8, name="scales", align_bytes=64)
+
+        def gather(into, window, a, n):
+            nc.vector.tensor_copy(into[:, a:a + n], window[:].indirect(offs_sb[:, a // 16:(a + n) // 16]))
+
+        def multiply(e, a, b, name, copy):
+            acc = psum.tile([P, b - a], F32, name=name)
+            nc.tensor.matmul_mx(
+                out=acc[:],
+                lhsT=w_codes[:, e, :].bitcast(FP8X4),
+                lhsT_scale=w_bytes[:, e, :],
+                rhs=words[:, a:b].bitcast(FP8X4),
+                rhs_scale=scales[:, a:b],
+                start=True,
+                stop=True,
+            )
+            copy(out=y[:, a:b], in_=acc[:])
+
+        for a, n in ((0, 768), (768, 768)):
+            gather(scales, x_scales, a, n)
+            gather(words, x_words, a, n)
+            for e in range(a // C, (a + n) // C):
+                multiply(e, e * C, (e + 1) * C, "acc%d" % e, nc.scalar.copy)
+        gather(scales, x_scales, 1536, 512)
+        gather(words, x_words, 1536, 256)
+        multiply(6, 1536, 1792, "acc6", nc.scalar.copy)
+        gather(words, x_words, 1792, 256)
+        multiply(7, 1792, 1920, "acc7", nc.scalar.copy)
+        multiply(7, 1920, 2048, "acc0", nc.vector.tensor_copy)
+
+        first = keep.tile([P, T], F32, name="first")
+        nc.vector.tensor_tensor(first[:], y[:].indirect(pos1_sb[:]), gates[:, 0, :], MULT)
+        t0 = 0
+        for i, n in enumerate(SECOND):
+            second = keep.tile([P, n], F32, name="second%d" % i)
+            result = keep.tile([P, n], F32, name="result%d" % i)
+            nc.vector.tensor_tensor(second[:], y[:].indirect(pos2_sb[:, t0 // 16:(t0 + n) // 16]), gates[:, 1, t0:t0 + n], MULT)
+            nc.vector.tensor_tensor(result[:], first[:, t0:t0 + n], second[:], ADD)
+            nc.sync.dma_start(out=out[:, t0:t0 + n], in_=result[:])
+            t0 += n

@@ -1,3 +1,4 @@
+import concourse.masks as masks
 import concourse.mybir as mybir
 
 F32 = mybir.dt.float32
@@ -17,20 +18,22 @@ FLOPS = 2 * K * N * SLOTS
 
 LOADS = (256, 256, 256, 128, 128)
 SCALAR_SHARE = (96, 96, 96, 48, 48)
-SECOND = (512, 384, 128)
+ON_TENSOR = 256
+CHUNKS = ((256, 768), (768, 896), (896, 1024))
 
 
 def tile_routed_moe_kernel(tc, xT, w_words, w_scales, gate, offs, pos1, pos2, out):
     nc = tc.nc
     with (
         tc.tile_pool(name="keep", bufs=1) as keep,
+        tc.tile_pool(name="ring", bufs=2) as ring,
         tc.psum_pool(name="psum", bufs=1) as psum,
     ):
         offs_sb = keep.tile([P, SLOTS // 16], U16, name="offs_sb")
         pos1_sb = keep.tile([P, T // 16], U16, name="pos1_sb")
         pos2_sb = keep.tile([P, T // 16], U16, name="pos2_sb")
         x_words = keep.tile([P, T], U32, name="x_words", align_bytes=64)
-        x_scales = keep.tile([P, T], U8, name="x_scales", align_bytes=64)
+        x_scales = keep.tile([P, 2 * T], U8, name="x_scales", align_bytes=64)
         w_codes = keep.tile([P, E, N], I32, name="w_codes", align_bytes=64)
         w_bytes = keep.tile([P, E, N], U8, name="w_bytes", align_bytes=64)
         gates = keep.tile([P, 2, T], F32, name="gates")
@@ -41,6 +44,8 @@ def tile_routed_moe_kernel(tc, xT, w_words, w_scales, gate, offs, pos1, pos2, ou
         nc.gpsimd.memset(warm[:], 0.0)
         nc.scalar.copy(warm2[:], warm[:])
         nc.gpsimd.memset(x_scales[:], 0)
+        identity = keep.tile([P, P], F32, name="identity")
+        masks.make_identity(nc, identity[:])
         nc.vector.memset(w_bytes[:].bitcast(I32), 0)
 
         x_rows = xT.rearrange("(p t) n -> p t n", t=4)
@@ -99,8 +104,8 @@ def tile_routed_moe_kernel(tc, xT, w_words, w_scales, gate, offs, pos1, pos2, ou
             )
             copy(out=y[:, a:b], in_=acc[:])
 
+        gather(scales, x_scales, 0, 1536)
         for a, n in ((0, 768), (768, 768)):
-            gather(scales, x_scales, a, n)
             gather(words, x_words, a, n)
             for e in range(a // C, (a + n) // C):
                 multiply(e, e * C, (e + 1) * C, "acc%d" % e, nc.scalar.copy)
@@ -108,16 +113,26 @@ def tile_routed_moe_kernel(tc, xT, w_words, w_scales, gate, offs, pos1, pos2, ou
         gather(words, x_words, 1536, 256)
         multiply(6, 1536, 1792, "acc6", nc.scalar.copy)
         gather(words, x_words, 1792, 256)
-        multiply(7, 1792, 1920, "acc7", nc.scalar.copy)
-        multiply(7, 1920, 2048, "acc0", nc.vector.tensor_copy)
+        multiply(7, 1792, 1920, "acc7", nc.vector.tensor_copy)
+        multiply(7, 1920, 2048, "acc0", nc.scalar.copy)
 
         first = keep.tile([P, T], F32, name="first")
-        nc.vector.tensor_tensor(first[:], y[:].indirect(pos1_sb[:]), gates[:, 0, :], MULT)
-        t0 = 0
-        for i, n in enumerate(SECOND):
-            second = keep.tile([P, n], F32, name="second%d" % i)
-            result = keep.tile([P, n], F32, name="result%d" % i)
-            nc.vector.tensor_tensor(second[:], y[:].indirect(pos2_sb[:, t0 // 16:(t0 + n) // 16]), gates[:, 1, t0:t0 + n], MULT)
-            nc.vector.tensor_tensor(result[:], first[:, t0:t0 + n], second[:], ADD)
-            nc.sync.dma_start(out=out[:, t0:t0 + n], in_=result[:])
-            t0 += n
+        second = keep.tile([P, ON_TENSOR], F32, name="second")
+        result = keep.tile([P, T], F32, name="result")
+
+        def fetch(products, positions, which, a, b):
+            nc.vector.tensor_tensor(products[:, a:b], y[:].indirect(positions[:, a // 16:b // 16]), gates[:, which, a:b], MULT)
+
+        fetch(first, pos1_sb, 0, 0, ON_TENSOR)
+        sums = psum.tile([P, ON_TENSOR], F32, name="acc1")
+        nc.tensor.matmul(sums[:], identity[:], first[:, :ON_TENSOR], start=True, stop=False)
+        fetch(second, pos2_sb, 1, 0, ON_TENSOR)
+        nc.tensor.matmul(sums[:], identity[:], second[:, :ON_TENSOR], start=False, stop=True)
+        nc.scalar.copy(out=result[:, :ON_TENSOR], in_=sums[:])
+        nc.sync.dma_start(out=out[:, :ON_TENSOR], in_=result[:, :ON_TENSOR])
+        fetch(first, pos1_sb, 0, ON_TENSOR, T)
+        for a, b in CHUNKS:
+            late = ring.tile([P, b - a], F32, name="late")
+            nc.vector.tensor_tensor(late[:], y[:].indirect(pos2_sb[:, a // 16:b // 16]), gates[:, 1, a:b], MULT)
+            nc.vector.tensor_tensor(result[:, a:b], first[:, a:b], late[:], ADD)
+            nc.sync.dma_start(out=out[:, a:b], in_=result[:, a:b])

@@ -16,8 +16,8 @@ K, T, E, C, N = 512, 1024, 8, 256, 128
 SLOTS = E * C
 FLOPS = 2 * K * N * SLOTS
 
-LOADS = (256, 256, 256, 128, 128)
-SCALAR_SHARE = (96, 96, 96, 48, 48)
+LOADS = (512, 256, 128, 128)
+SCALAR_SHARE = (240, 112, 56, 56)
 ON_TENSOR = 256
 CHUNKS = ((256, 768), (768, 896), (896, 1024))
 

@@ -16,8 +16,8 @@ K, T, E, C, N = 512, 1024, 8, 256, 128
 SLOTS = E * C
 FLOPS = 2 * K * N * SLOTS
 
-LOADS = (512, 256, 128, 128)
-SCALAR_SHARE = (240, 112, 56, 56)
+LOADS = (512, 256, 256)
+PIECES = ((0, 0, 256, 144), (0, 256, 256, 144), (1, 0, 256, 144), (2, 0, 128, 64), (2, 128, 128, 48))
 ON_TENSOR = 256
 CHUNKS = ((256, 768), (768, 896), (896, 1024))
 
@@ -69,15 +69,13 @@ def tile_routed_moe_kernel(tc, xT, w_words, w_scales, gate, offs, pos1, pos2, ou
         nc.sync.dma_start(out=gates[:, 1, :], in_=gate[1])
 
         t0 = 0
-        for i, n in enumerate(LOADS):
+        for i, (load, start, n, s) in enumerate(PIECES):
             pairs = keep.tile([P, n, 4], BF16, name="pairs%d" % i, align_bytes=64)
-            s = SCALAR_SHARE[i]
             for copy, a, b in ((nc.scalar.copy, 0, s), (nc.vector.tensor_copy, s, n)):
-                if b > a:
-                    copy(
-                        out=pairs[:, a:b, :].rearrange("p (c i) t -> p c t i", i=4),
-                        in_=raws[i][:, :, a:b].rearrange("p t (c i) -> p c t i", i=4),
-                    )
+                copy(
+                    out=pairs[:, a:b, :].rearrange("p (c i) t -> p c t i", i=4),
+                    in_=raws[load][:, :, start + a:start + b].rearrange("p t (c i) -> p c t i", i=4),
+                )
             nc.vector.quantize_mx(
                 out=x_words[:, t0:t0 + n].bitcast(FP8X4),
                 scales=x_scales[:, t0:t0 + n],

import concourse.masks as masks
import concourse.mybir as mybir

F32 = mybir.dt.float32
BF16 = mybir.dt.bfloat16
I32 = mybir.dt.int32
U32 = mybir.dt.uint32
U16 = mybir.dt.uint16
U8 = mybir.dt.uint8
FP8X4 = mybir.dt.float8_e4m3fn_x4
MULT = mybir.AluOpType.mult
ADD = mybir.AluOpType.add

P = 128
K, T, E, C, N = 512, 1024, 8, 256, 128
SLOTS = E * C
FLOPS = 2 * K * N * SLOTS

LOADS = (512, 256, 256)
PIECES = ((0, 0, 256, 144), (0, 256, 256, 144), (1, 0, 256, 144), (2, 0, 128, 64), (2, 128, 128, 48))
ON_TENSOR = 256
CHUNKS = ((256, 768), (768, 896), (896, 1024))


def tile_routed_moe_kernel(tc, xT, w_words, w_scales, gate, offs, pos1, pos2, out):
    nc = tc.nc
    with (
        tc.tile_pool(name="keep", bufs=1) as keep,
        tc.tile_pool(name="ring", bufs=2) as ring,
        tc.psum_pool(name="psum", bufs=1) as psum,
    ):
        offs_sb = keep.tile([P, SLOTS // 16], U16, name="offs_sb")
        pos1_sb = keep.tile([P, T // 16], U16, name="pos1_sb")
        pos2_sb = keep.tile([P, T // 16], U16, name="pos2_sb")
        x_words = keep.tile([P, T], U32, name="x_words", align_bytes=64)
        x_scales = keep.tile([P, 2 * T], U8, name="x_scales", align_bytes=64)
        w_codes = keep.tile([P, E, N], I32, name="w_codes", align_bytes=64)
        w_bytes = keep.tile([P, E, N], U8, name="w_bytes", align_bytes=64)
        gates = keep.tile([P, 2, T], F32, name="gates")
        y = keep.tile([P, SLOTS], F32, name="y")
        warm = keep.tile([P, 16], F32, name="warm")
        warm2 = keep.tile([P, 16], F32, name="warm2")

        nc.gpsimd.memset(warm[:], 0.0)
        nc.scalar.copy(warm2[:], warm[:])
        nc.gpsimd.memset(x_scales[:], 0)
        identity = keep.tile([P, P], F32, name="identity")
        masks.make_identity(nc, identity[:])
        nc.vector.memset(w_bytes[:].bitcast(I32), 0)

        x_rows = xT.rearrange("(p t) n -> p t n", t=4)
        t0 = 0
        raws = []
        for i, n in enumerate(LOADS):
            raw = keep.tile([P, 4, n], F32, name="raw%d" % i)
            nc.sync.dma_start(out=raw[:], in_=x_rows[:, :, t0:t0 + n])
            raws.append(raw)
            t0 += n
        nc.sync.dma_start(offs_sb[:], offs)
        nc.sync.dma_start(out=w_codes[:], in_=w_words[:, 0].rearrange("e p n r -> p e (n r)").bitcast(I32))
        for q in range(4):
            nc.sync.dma_start(
                out=w_bytes[32 * q:32 * q + 4, :, :].bitcast(I32),
                in_=w_scales[:, 0, 4 * q:4 * q + 4, :].rearrange("e q n -> q e n").bitcast(I32),
            )
        nc.sync.dma_start(pos1_sb[:], pos1)
        nc.sync.dma_start(out=gates[:, 0, :], in_=gate[0])
        nc.sync.dma_start(pos2_sb[:], pos2)
        nc.sync.dma_start(out=gates[:, 1, :], in_=gate[1])

        t0 = 0
        for i, (load, start, n, s) in enumerate(PIECES):
            pairs = keep.tile([P, n, 4], BF16, name="pairs%d" % i, align_bytes=64)
            for copy, a, b in ((nc.scalar.copy, 0, s), (nc.vector.tensor_copy, s, n)):
                copy(
                    out=pairs[:, a:b, :].rearrange("p (c i) t -> p c t i", i=4),
                    in_=raws[load][:, :, start + a:start + b].rearrange("p t (c i) -> p c t i", i=4),
                )
            nc.vector.quantize_mx(
                out=x_words[:, t0:t0 + n].bitcast(FP8X4),
                scales=x_scales[:, t0:t0 + n],
                in_=pairs[:].rearrange("p n t -> p (n t)"),
            )
            t0 += n

        words = keep.tile([P, SLOTS], U32, name="words", align_bytes=64)
        scales = keep.tile([P, SLOTS], U8, name="scales", align_bytes=64)

        def gather(into, window, a, n):
            nc.vector.tensor_copy(into[:, a:a + n], window[:].indirect(offs_sb[:, a // 16:(a + n) // 16]))

        def multiply(e, a, b, name, copy):
            acc = psum.tile([P, b - a], F32, name=name)
            nc.tensor.matmul_mx(
                out=acc[:],
                lhsT=w_codes[:, e, :].bitcast(FP8X4),
                lhsT_scale=w_bytes[:, e, :],
                rhs=words[:, a:b].bitcast(FP8X4),
                rhs_scale=scales[:, a:b],
                start=True,
                stop=True,
            )
            copy(out=y[:, a:b], in_=acc[:])

        gather(scales, x_scales, 0, 1536)
        for a, n in ((0, 768), (768, 768)):
            gather(words, x_words, a, n)
            for e in range(a // C, (a + n) // C):
                multiply(e, e * C, (e + 1) * C, "acc%d" % e, nc.scalar.copy)
        gather(scales, x_scales, 1536, 512)
        gather(words, x_words, 1536, 256)
        multiply(6, 1536, 1792, "acc6", nc.scalar.copy)
        gather(words, x_words, 1792, 256)
        multiply(7, 1792, 1920, "acc7", nc.vector.tensor_copy)
        multiply(7, 1920, 2048, "acc0", nc.scalar.copy)

        first = keep.tile([P, T], F32, name="first")
        second = keep.tile([P, ON_TENSOR], F32, name="second")
        result = keep.tile([P, T], F32, name="result")

        def fetch(products, positions, which, a, b):
            nc.vector.tensor_tensor(products[:, a:b], y[:].indirect(positions[:, a // 16:b // 16]), gates[:, which, a:b], MULT)

        fetch(first, pos1_sb, 0, 0, ON_TENSOR)
        sums = psum.tile([P, ON_TENSOR], F32, name="acc1")
        nc.tensor.matmul(sums[:], identity[:], first[:, :ON_TENSOR], start=True, stop=False)
        fetch(second, pos2_sb, 1, 0, ON_TENSOR)
        nc.tensor.matmul(sums[:], identity[:], second[:, :ON_TENSOR], start=False, stop=True)
        nc.scalar.copy(out=result[:, :ON_TENSOR], in_=sums[:])
        nc.sync.dma_start(out=out[:, :ON_TENSOR], in_=result[:, :ON_TENSOR])
        fetch(first, pos1_sb, 0, ON_TENSOR, T)
        for a, b in CHUNKS:
            late = ring.tile([P, b - a], F32, name="late")
            nc.vector.tensor_tensor(late[:], y[:].indirect(pos2_sb[:, a // 16:b // 16]), gates[:, 1, a:b], MULT)
            nc.vector.tensor_tensor(result[:, a:b], first[:, a:b], late[:], ADD)
            nc.sync.dma_start(out=out[:, a:b], in_=result[:, a:b])
